import numpy as np
import ml_dtypes


def mxq(x, axis, fmt="e4m3"):
    dtype, down = {"e4m3": (ml_dtypes.float8_e4m3fn, 7), "e5m2": (ml_dtypes.float8_e5m2, 14)}[fmt]
    v = np.moveaxis(np.asarray(x, np.float32).astype(ml_dtypes.bfloat16).astype(np.float64), axis, -1)
    blocks = v.reshape(v.shape[:-1] + (-1, 32))
    amax = np.abs(blocks).max(-1, keepdims=True)
    byte = np.maximum(np.where(amax > 0, np.frexp(amax)[1] - 1 + 127, 0) - down, 1)
    scale = np.exp2(byte - 127.0)
    codes = (blocks / scale).astype(np.float32).astype(dtype).astype(np.float64)
    return np.moveaxis((codes * scale).reshape(v.shape), -1, axis)


WIDE = False


def mx_kscale(k):
    if not WIDE:
        return np.ones(k)
    levels = np.array([10, -10, 5, -5, 0])
    if k % 512:
        return np.exp2(np.random.permutation(np.resize(levels, k // 32))).repeat(32)
    a = np.empty((k // 512, 16))
    for p in range(k // 512):
        a[p, :8] = np.random.permutation(np.resize(levels, 8))
        for g in range(8):
            far = levels[np.abs(levels - a[p, g]) >= 10]
            a[p, g + 8] = far[np.random.randint(len(far))]
    return np.exp2(a.ravel()).repeat(32)


def f64(x):
    return np.asarray(x).astype(np.float64)


def striped(idx):
    return np.tile(idx.reshape(-1, 16).T, (8, 1)).astype(np.uint16)


def unstriped(offs):
    return offs[:16].T.reshape(-1).astype(np.int64)


def striped8(idx):
    return np.concatenate([x.reshape(-1, 16).T for x in idx]).astype(np.uint16)


def runs(offs, k):
    lists = np.stack([offs[16 * r : 16 * r + 16].T.reshape(-1) for r in range(8)]).astype(np.int64)
    return lists[np.arange(k) % 512 // 64]


def pack_weight(w):
    k, n = w.shape
    w = f64(np.asarray(w, np.float32).astype(ml_dtypes.bfloat16)).reshape(k // 32, 32, n)
    amax = np.abs(w).max(1)
    byte = np.clip(np.where(amax > 0, np.frexp(amax)[1] - 1 + 127 - 7, 1), 1, 254)
    scaled = (w * np.exp2(127.0 - byte)[:, None, :]).reshape(k, n).astype(np.float32)
    words = np.ascontiguousarray(scaled.reshape(k // 512, 128, 4, n).transpose(0, 1, 3, 2)).astype(ml_dtypes.float8_e4m3fn).view(np.uint8)
    return words, np.ascontiguousarray(byte.astype(np.uint8).reshape(k // 512, 16, n))


def unpack_weight(words, scales):
    g, p, n, _ = words.shape
    vals = np.ascontiguousarray(words).view(ml_dtypes.float8_e4m3fn).astype(np.float64) * np.repeat(np.exp2(scales.astype(np.float64) - 127.0), 8, axis=1)[..., None]
    return vals.transpose(0, 1, 3, 2).reshape(g * 512, n)


K, T, S, H, G, W = 512, 1024, 512, 512, 2048, 256


def setup_inputs():
    n = np.random.standard_normal
    s = mx_kscale(K)[:, None]
    packed_xT = pack_weight(n((K, T)) * s)
    packed_dT = pack_weight(n((K, G)) / s)
    perm = np.stack([np.random.permutation(S) for _ in range(8)])
    return {
        "x_words": packed_xT[0],
        "x_scales": packed_xT[1],
        "w1": (n((K, H)) / np.sqrt(K) / s).astype(np.float32),
        "w2": (n((K, H)) / np.sqrt(K) / s).astype(np.float32),
        "gs": (np.random.uniform(0.5, 1.5, (K, 1)) * s).astype(np.float32),
        "d_words": packed_dT[0],
        "d_scales": packed_dT[1],
        "offs": striped(np.random.permutation(T)[:S]),
        "two": striped(np.random.permutation(T)[:S]),
        "n1": striped8(np.stack([np.random.permutation(S) for _ in range(8)])),
        "n2": striped8(np.stack([np.random.permutation(S) for _ in range(8)])),
        "k1": striped8(np.random.randint(0, G, (8, H))),
        "n3": striped8(perm[:, :W]),
        "n4": striped8(perm[:, W:]),
    }


def reference(x_words, x_scales, w1, w2, gs, d_words, d_scales, offs, two, n1, n2, k1, n3, n4):
    d_k1 = unpack_weight(d_words, d_scales)[np.arange(K)[:, None], runs(k1, K)]
    xq = unpack_weight(x_words, x_scales)[:, unstriped(offs)]
    y = mxq(f64(w1), 0, "e4m3").T @ xq
    x_two = unpack_weight(x_words, x_scales)[:, unstriped(two)]
    d = mxq(f64(w2), 0, "e4m3").T @ x_two
    z = f64(gs) * ((y - (y[np.arange(H)[:, None], runs(n1, H)])) / (np.abs(d) + np.abs(d[np.arange(H)[:, None], runs(n2, H)]) + 0.5))
    h = 0.0625 * ((d_k1.T @ mxq(z, 0, "e4m3")))
    pa = h[np.arange(H)[:, None], runs(n3, H)]
    pb = h[np.arange(H)[:, None], runs(n4, H)]
    rb = np.maximum(pa, pb)
    ra = pa / (np.abs(pb) + 0.5)
    ds = np.zeros((H, S))
    ds[np.arange(H)[:, None], runs(n3, H)] = ra
    out = ds.copy()
    out[np.arange(H)[:, None], runs(n4, H)] = rb
    return out

@@ -1,0 +1,209 @@
+from contextlib import ExitStack
+
+import concourse.mybir as mybir
+
+F32 = mybir.dt.float32
+BF16 = mybir.dt.bfloat16
+I32 = mybir.dt.int32
+U32 = mybir.dt.uint32
+U16 = mybir.dt.uint16
+U8 = mybir.dt.uint8
+FP8X4 = mybir.dt.float8_e4m3fn_x4
+ALU = mybir.AluOpType
+ACT = mybir.ActivationFunctionType
+
+P = 128
+PACK = 4
+K, T, S, H, G, W = 512, 1024, 512, 512, 2048, 256
+FLOPS = 3 * 2 * K * H * S
+Z_CHUNKS = ((0, 256), (256, 384), (384, 512))
+
+
+def tile_picked_twqnormbratio_none_p_kernel(tc, x_words, x_scales, w1, w2, gs, d_words, d_scales, offs, two, n1, n2, k1, n3, n4, out):
+    nc = tc.nc
+    with ExitStack() as ctx:
+        lists = ctx.enter_context(tc.tile_pool(name="lists", bufs=1))
+        sb = ctx.enter_context(tc.tile_pool(name="sb", bufs=1))
+        psum = ctx.enter_context(tc.psum_pool(name="psum", bufs=1))
+
+        def tile(name, shape, dtype):
+            return sb.tile(shape, dtype, name=name, align_bytes=64)
+
+        def load_list(name, src):
+            dst = lists.tile(list(src.shape), U16, name=name)
+            nc.sync.dma_start(dst[:], src)
+            return dst
+
+        warm = tile("warm", [P, 1], F32)
+        warm2 = tile("warm2", [P, 1], F32)
+        nc.gpsimd.memset(warm[:], 1.0)
+        nc.scalar.activation(warm2[:], warm[:], ACT.Abs_reciprocal_sqrt)
+
+        xs_tab = tile("xs_tab", [P, T], U8)
+        nc.vector.memset(xs_tab[:].bitcast(I32), 0)
+        ds_tab = tile("ds_tab", [P, G], U8)
+        nc.vector.memset(ds_tab[:].bitcast(I32), 0)
+        dk_scales = tile("dk_scales", [P, H], U8)
+        nc.vector.memset(dk_scales[:].bitcast(I32), 0)
+
+        two_sb = load_list("two_sb", two)
+        for q in range(4):
+            nc.sync.dma_start(xs_tab[32 * q : 32 * q + 4, :].bitcast(I32), x_scales[0, 4 * q : 4 * q + 4, :].bitcast(I32))
+        offs_sb = load_list("offs_sb", offs)
+        xw_tab = tile("xw_tab", [P, T], U32)
+        nc.sync.dma_start(xw_tab[:].bitcast(I32), x_words[0].rearrange("p n r -> p (n r)").bitcast(I32))
+
+        def load_weight(name, w):
+            halves = []
+            for u in range(2):
+                raw = tile("%s_raw%d" % (name, u), [P, PACK, H // 2], F32)
+                nc.sync.dma_start(raw[:], w.rearrange("(p j) c -> p j c", j=PACK)[:, :, u * 256 : (u + 1) * 256])
+                halves.append(raw)
+            return halves
+
+        w2_raw = load_weight("w2", w2)
+        k1_sb = load_list("k1_sb", k1)
+        for s in range(2):
+            nc.sync.dma_start(ds_tab[s:P:16, :].bitcast(I32), d_scales[0, s:16:2, :].bitcast(I32))
+        dw_tab = tile("dw_tab", [P, G], U32)
+        nc.sync.dma_start(dw_tab[:].bitcast(I32), d_words[0].rearrange("p n r -> p (n r)").bitcast(I32))
+        w1_raw = load_weight("w1", w1)
+        n2_sb = load_list("n2_sb", n2)
+        gs_sb = tile("gs_sb", [P, PACK], F32)
+        nc.sync.dma_start(gs_sb[:], gs.rearrange("(p t) o -> p (t o)", t=PACK))
+        n1_sb = load_list("n1_sb", n1)
+        n3_sb = load_list("n3_sb", n3)
+        n4_sb = load_list("n4_sb", n4)
+        neg_gs = tile("neg_gs", [P, PACK], F32)
+        nc.gpsimd.tensor_scalar(neg_gs[:], gs_sb[:], -1.0, 0.0, ALU.mult, ALU.add)
+
+        def gather(name, table, offsets, n, dtype):
+            dst = tile(name, [P, n], dtype)
+            nc.vector.tensor_copy(dst[:], table[:].indirect(offsets[:]))
+            return dst
+
+        x2_scales = gather("x2_scales", xs_tab, two_sb, S, U8)
+        x1_scales = gather("x1_scales", xs_tab, offs_sb, S, U8)
+        x2_words = gather("x2_words", xw_tab, two_sb, S, U32)
+        x1_words = gather("x1_words", xw_tab, offs_sb, S, U32)
+
+        def round_weight(name, halves):
+            wb = tile(name + "_bf", [P, PACK, P, PACK], BF16)
+            for u in range(2):
+                nc.scalar.copy(
+                    wb[:, :, u * 64 : (u + 1) * 64, :].rearrange("p t m j -> p m j t"),
+                    halves[u][:].rearrange("p j (m t) -> p m j t", t=PACK),
+                )
+            return wb
+
+        def quantize(name, src, n):
+            codes = tile(name + "_codes", [P, n], U32)
+            scales = tile(name + "_scales", [P, n], U8)
+            nc.vector.quantize_mx(out=codes[:].bitcast(FP8X4), scales=scales[:], in_=src)
+            return codes, scales
+
+        def product(dst, lhs, t, rhs):
+            cols = slice(t * P, (t + 1) * P)
+            nc.tensor.matmul_mx(
+                out=dst,
+                lhsT=lhs[0][:, cols].bitcast(FP8X4),
+                lhsT_scale=lhs[1][:, cols],
+                rhs=rhs[0][:].bitcast(FP8X4),
+                rhs_scale=rhs[1][:],
+                start=True,
+                stop=True,
+            )
+
+        windows = [tile("win%d" % g, [P, S if g in (0, 8) else 2 * S], F32) for g in range(9)]
+
+        def own(g):
+            return windows[g][:, 0:S]
+
+        def spare(g):
+            return windows[g + 1][:, (0 if g == 7 else S) :]
+
+        w2_bf = round_weight("w2", w2_raw)
+        w2_q = quantize("w2", w2_bf[:].rearrange("p t m j -> p (t m j)"), H)
+        d_ps = [psum.tile([P, S], F32, name="d_ps%d" % t, tag="a%d" % t) for t in range(PACK)]
+        for t in range(PACK):
+            product(d_ps[t][:], w2_q, t, (x2_words, x2_scales))
+        for t in range(PACK):
+            nc.scalar.activation(own(t), d_ps[t][:], ACT.Abs)
+            if t == 0:
+                nc.scalar.activation(spare(t), d_ps[t][:], ACT.Abs)
+            else:
+                nc.sync.dma_start(spare(t), own(t))
+
+        dk_raw_scales = gather("dk_raw_scales", ds_tab, k1_sb, H, U8)
+        dk_dealt = tile("dk_dealt", [P, H], U8)
+        nc.vector.tensor_copy(
+            dk_dealt[:].rearrange("p (t m) -> p m t", t=PACK), dk_raw_scales[:].rearrange("p (m t) -> p m t", t=PACK)
+        )
+        for r in range(4):
+            nc.sync.dma_start(dk_scales[r:P:32, :].bitcast(I32), dk_dealt[16 * (r // 2) + r % 2 : P : 32, :].bitcast(I32))
+        dk_raw_words = gather("dk_raw_words", dw_tab, k1_sb, H, U32)
+        dk_words = tile("dk_words", [P, H], U32)
+        nc.vector.tensor_copy(
+            dk_words[:].rearrange("p (t m) -> p m t", t=PACK), dk_raw_words[:].rearrange("p (m t) -> p m t", t=PACK)
+        )
+
+        w1_bf = round_weight("w1", w1_raw)
+        w1_q = quantize("w1", w1_bf[:].rearrange("p t m j -> p (t m j)"), H)
+        y_ps = [psum.tile([P, S], F32, name="y_ps%d" % t, tag="b%d" % t) for t in range(PACK)]
+        for t in range(PACK):
+            product(y_ps[t][:], w1_q, t, (x1_words, x1_scales))
+
+        den = tile("den", [P, PACK, S], F32)
+        root = tile("root", [P, PACK, S], F32)
+        inv = tile("inv", [P, PACK, S], F32)
+        num = tile("num", [P, PACK, S], F32)
+        for t in range(PACK):
+            if t == 0:
+                for u in range(2):
+                    cols = slice(u * 256, (u + 1) * 256)
+                    nc.vector.tensor_tensor(
+                        den[:, t, cols], windows[t][:].indirect(n2_sb[:, u * 16 : (u + 1) * 16]), spare(t)[:, cols], ALU.add
+                    )
+            else:
+                nc.vector.tensor_tensor(den[:, t, :], windows[t][:].indirect(n2_sb[:]), spare(t), ALU.add)
+        for t in range(PACK):
+            nc.scalar.activation(own(PACK + t), y_ps[t][:], ACT.Copy, scale=neg_gs[:, t : t + 1])
+            nc.sync.dma_start(spare(PACK + t), own(PACK + t))
+        for t in range(PACK):
+            nc.scalar.activation(root[:, t, :], den[:, t, :], ACT.Abs_reciprocal_sqrt, bias=0.5)
+            nc.scalar.activation(inv[:, t, :], root[:, t, :], ACT.Square)
+        for t in range(PACK):
+            nc.vector.tensor_tensor(num[:, t, :], windows[PACK + t][:].indirect(n1_sb[:]), spare(PACK + t), ALU.subtract)
+
+        h_ps = [psum.tile([P, S], F32, name="h_ps%d" % t, tag="a%d" % t) for t in range(PACK)]
+        h_sb = [tile("h_sb%d" % t, [P, S], F32) for t in range(PACK)]
+        for c, (lo, hi) in enumerate(Z_CHUNKS):
+            z_bf = tile("z_bf%d" % c, [P, hi - lo, PACK], BF16)
+            nc.vector.tensor_tensor(
+                z_bf[:].rearrange("p (c i) t -> p c t i", i=4),
+                num[:, :, lo:hi].rearrange("p t (c i) -> p c t i", i=4),
+                inv[:, :, lo:hi].rearrange("p t (c i) -> p c t i", i=4),
+                ALU.mult,
+            )
+            z_q = quantize("z%d" % c, z_bf[:].rearrange("p n t -> p (n t)"), hi - lo)
+            for t in range(PACK):
+                product(h_ps[t][:, lo:hi], (dk_words, dk_scales), t, z_q)
+        for t in range(PACK):
+            nc.scalar.activation(h_sb[t][:], h_ps[t][:], ACT.Copy, scale=0.0625)
+
+        out_rows = out.rearrange("(p t) n -> t p n", t=PACK)
+        for t in range(PACK):
+            pb = gather("pb%d" % t, h_sb[t], n4_sb, W, F32)
+            pa = gather("pa%d" % t, h_sb[t], n3_sb, W, F32)
+            size = tile("size%d" % t, [P, W], F32)
+            nc.scalar.activation(size[:], pb[:], ACT.Abs)
+            rt = tile("rt%d" % t, [P, W], F32)
+            nc.scalar.activation(rt[:], size[:], ACT.Abs_reciprocal_sqrt, bias=0.5)
+            iv = tile("iv%d" % t, [P, W], F32)
+            nc.scalar.activation(iv[:], rt[:], ACT.Square)
+            rb = tile("rb%d" % t, [P, W], F32)
+            nc.vector.tensor_tensor(rb[:], pa[:], pb[:], ALU.max)
+            res = tile("res%d" % t, [P, S], F32)
+            nc.vector.tensor_copy(res[:].indirect(n4_sb[:]), rb[:])
+            nc.vector.tensor_tensor(res[:].indirect(n3_sb[:]), pa[:], iv[:], ALU.mult)
+            nc.sync.dma_start(out_rows[t], res[:])

@@ -34,43 +34,38 @@ def tile_picked_twqnormbratio_none_p_kernel(tc, x_words, x_scales, w1, w2, gs, d
             nc.sync.dma_start(dst[:], src)
             return dst
 
+        xs_tab = tile("xs_tab", [P, T], U8)
+        nc.gpsimd.memset(xs_tab[:].bitcast(I32), 0)
         warm = tile("warm", [P, 1], F32)
         warm2 = tile("warm2", [P, 1], F32)
-        nc.gpsimd.memset(warm[:], 1.0)
+        nc.vector.memset(warm[:], 1.0)
         nc.scalar.activation(warm2[:], warm[:], ACT.Abs_reciprocal_sqrt)
-
-        xs_tab = tile("xs_tab", [P, T], U8)
-        nc.vector.memset(xs_tab[:].bitcast(I32), 0)
         ds_tab = tile("ds_tab", [P, G], U8)
         nc.vector.memset(ds_tab[:].bitcast(I32), 0)
-        dk_scales = tile("dk_scales", [P, H], U8)
-        nc.vector.memset(dk_scales[:].bitcast(I32), 0)
+
+        def load_half(name, w, u):
+            raw = tile("%s_raw%d" % (name, u), [P, PACK, H // 2], F32)
+            nc.sync.dma_start(raw[:], w.rearrange("(p j) c -> p j c", j=PACK)[:, :, u * 256 : (u + 1) * 256])
+            return raw
 
         two_sb = load_list("two_sb", two)
+        offs_sb = load_list("offs_sb", offs)
         for q in range(4):
             nc.sync.dma_start(xs_tab[32 * q : 32 * q + 4, :].bitcast(I32), x_scales[0, 4 * q : 4 * q + 4, :].bitcast(I32))
-        offs_sb = load_list("offs_sb", offs)
+        w2_raw = [load_half("w2", w2, 0)]
         xw_tab = tile("xw_tab", [P, T], U32)
         nc.sync.dma_start(xw_tab[:].bitcast(I32), x_words[0].rearrange("p n r -> p (n r)").bitcast(I32))
-
-        def load_weight(name, w):
-            halves = []
-            for u in range(2):
-                raw = tile("%s_raw%d" % (name, u), [P, PACK, H // 2], F32)
-                nc.sync.dma_start(raw[:], w.rearrange("(p j) c -> p j c", j=PACK)[:, :, u * 256 : (u + 1) * 256])
-                halves.append(raw)
-            return halves
-
-        w2_raw = load_weight("w2", w2)
+        w2_raw.append(load_half("w2", w2, 1))
+        w1_raw = [load_half("w1", w1, 0)]
         k1_sb = load_list("k1_sb", k1)
         for s in range(2):
             nc.sync.dma_start(ds_tab[s:P:16, :].bitcast(I32), d_scales[0, s:16:2, :].bitcast(I32))
-        dw_tab = tile("dw_tab", [P, G], U32)
-        nc.sync.dma_start(dw_tab[:].bitcast(I32), d_words[0].rearrange("p n r -> p (n r)").bitcast(I32))
-        w1_raw = load_weight("w1", w1)
+        w1_raw.append(load_half("w1", w1, 1))
         n2_sb = load_list("n2_sb", n2)
         gs_sb = tile("gs_sb", [P, PACK], F32)
         nc.sync.dma_start(gs_sb[:], gs.rearrange("(p t) o -> p (t o)", t=PACK))
+        dw_tab = tile("dw_tab", [P, G], U32)
+        nc.sync.dma_start(dw_tab[:].bitcast(I32), d_words[0].rearrange("p n r -> p (n r)").bitcast(I32))
         n1_sb = load_list("n1_sb", n1)
         n3_sb = load_list("n3_sb", n3)
         n4_sb = load_list("n4_sb", n4)
@@ -94,7 +89,10 @@ def tile_picked_twqnormbratio_none_p_kernel(tc, x_words, x_scales, w1, w2, gs, d
                     wb[:, :, u * 64 : (u + 1) * 64, :].rearrange("p t m j -> p m j t"),
                     halves[u][:].rearrange("p j (m t) -> p m j t", t=PACK),
                 )
-            return wb
+            return wb[:].rearrange("p t m j -> p (t m j)")
+
+        w2_bf = round_weight("w2", w2_raw)
+        w1_bf = round_weight("w1", w1_raw)
 
         def quantize(name, src, n):
             codes = tile(name + "_codes", [P, n], U32)
@@ -114,44 +112,39 @@ def tile_picked_twqnormbratio_none_p_kernel(tc, x_words, x_scales, w1, w2, gs, d
                 stop=True,
             )
 
-        windows = [tile("win%d" % g, [P, S if g in (0, 8) else 2 * S], F32) for g in range(9)]
-
         def own(g):
             return windows[g][:, 0:S]
 
         def spare(g):
             return windows[g + 1][:, (0 if g == 7 else S) :]
 
-        w2_bf = round_weight("w2", w2_raw)
-        w2_q = quantize("w2", w2_bf[:].rearrange("p t m j -> p (t m j)"), H)
+        windows = [tile("win%d" % g, [P, S if g in (0, 8) else 2 * S], F32) for g in range(9)]
+        w2_q = quantize("w2", w2_bf, H)
         d_ps = [psum.tile([P, S], F32, name="d_ps%d" % t, tag="a%d" % t) for t in range(PACK)]
         for t in range(PACK):
             product(d_ps[t][:], w2_q, t, (x2_words, x2_scales))
         for t in range(PACK):
             nc.scalar.activation(own(t), d_ps[t][:], ACT.Abs)
-            if t == 0:
-                nc.scalar.activation(spare(t), d_ps[t][:], ACT.Abs)
-            else:
-                nc.sync.dma_start(spare(t), own(t))
+            nc.scalar.activation(spare(t), d_ps[t][:], ACT.Abs)
 
         dk_raw_scales = gather("dk_raw_scales", ds_tab, k1_sb, H, U8)
-        dk_dealt = tile("dk_dealt", [P, H], U8)
+        dk_scales = tile("dk_scales", [P, H], U8)
         nc.vector.tensor_copy(
-            dk_dealt[:].rearrange("p (t m) -> p m t", t=PACK), dk_raw_scales[:].rearrange("p (m t) -> p m t", t=PACK)
+            dk_scales[:].rearrange("p (t m) -> p m t", t=PACK), dk_raw_scales[:].rearrange("p (m t) -> p m t", t=PACK)
         )
-        for r in range(4):
-            nc.sync.dma_start(dk_scales[r:P:32, :].bitcast(I32), dk_dealt[16 * (r // 2) + r % 2 : P : 32, :].bitcast(I32))
+        for s in range(2):
+            nc.sync.dma_start(dk_scales[2 + s : P : 32, :].bitcast(I32), dk_scales[16 + s : P : 32, :].bitcast(I32))
+
+        w1_q = quantize("w1", w1_bf, H)
+        y_ps = [psum.tile([P, S], F32, name="y_ps%d" % t, tag="b%d" % t) for t in range(PACK)]
+        for t in range(PACK):
+            product(y_ps[t][:], w1_q, t, (x1_words, x1_scales))
+
         dk_raw_words = gather("dk_raw_words", dw_tab, k1_sb, H, U32)
         dk_words = tile("dk_words", [P, H], U32)
         nc.vector.tensor_copy(
             dk_words[:].rearrange("p (t m) -> p m t", t=PACK), dk_raw_words[:].rearrange("p (m t) -> p m t", t=PACK)
         )
-
-        w1_bf = round_weight("w1", w1_raw)
-        w1_q = quantize("w1", w1_bf[:].rearrange("p t m j -> p (t m j)"), H)
-        y_ps = [psum.tile([P, S], F32, name="y_ps%d" % t, tag="b%d" % t) for t in range(PACK)]
-        for t in range(PACK):
-            product(y_ps[t][:], w1_q, t, (x1_words, x1_scales))
 
         den = tile("den", [P, PACK, S], F32)
         root = tile("root", [P, PACK, S], F32)
@@ -168,28 +161,47 @@ def tile_picked_twqnormbratio_none_p_kernel(tc, x_words, x_scales, w1, w2, gs, d
                 nc.vector.tensor_tensor(den[:, t, :], windows[t][:].indirect(n2_sb[:]), spare(t), ALU.add)
         for t in range(PACK):
             nc.scalar.activation(own(PACK + t), y_ps[t][:], ACT.Copy, scale=neg_gs[:, t : t + 1])
-            nc.sync.dma_start(spare(PACK + t), own(PACK + t))
+            if t == 0:
+                nc.scalar.activation(spare(PACK + t), y_ps[t][:], ACT.Copy, scale=neg_gs[:, t : t + 1])
+            else:
+                nc.sync.dma_start(spare(PACK + t), own(PACK + t))
         for t in range(PACK):
             nc.scalar.activation(root[:, t, :], den[:, t, :], ACT.Abs_reciprocal_sqrt, bias=0.5)
             nc.scalar.activation(inv[:, t, :], root[:, t, :], ACT.Square)
         for t in range(PACK):
             nc.vector.tensor_tensor(num[:, t, :], windows[PACK + t][:].indirect(n1_sb[:]), spare(PACK + t), ALU.subtract)
 
-        h_ps = [psum.tile([P, S], F32, name="h_ps%d" % t, tag="a%d" % t) for t in range(PACK)]
+        h_ps = [psum.tile([P, S], F32, name="h_ps%d" % t, tag="a%d" % t) for t in range(1, PACK)]
+        h0_ps = [psum.tile([P, S], F32, name="h0_ps%d" % c, tag="b%d" % c) for c in range(len(Z_CHUNKS))]
         h_sb = [tile("h_sb%d" % t, [P, S], F32) for t in range(PACK)]
-        for c, (lo, hi) in enumerate(Z_CHUNKS):
-            z_bf = tile("z_bf%d" % c, [P, hi - lo, PACK], BF16)
+        z_bf = []
+
+        def weigh(c):
+            lo, hi = Z_CHUNKS[c]
+            z = tile("z_bf%d" % c, [P, hi - lo, PACK], BF16)
             nc.vector.tensor_tensor(
-                z_bf[:].rearrange("p (c i) t -> p c t i", i=4),
+                z[:].rearrange("p (c i) t -> p c t i", i=4),
                 num[:, :, lo:hi].rearrange("p t (c i) -> p c t i", i=4),
                 inv[:, :, lo:hi].rearrange("p t (c i) -> p c t i", i=4),
                 ALU.mult,
             )
-            z_q = quantize("z%d" % c, z_bf[:].rearrange("p n t -> p (n t)"), hi - lo)
-            for t in range(PACK):
-                product(h_ps[t][:, lo:hi], (dk_words, dk_scales), t, z_q)
-        for t in range(PACK):
-            nc.scalar.activation(h_sb[t][:], h_ps[t][:], ACT.Copy, scale=0.0625)
+            z_bf.append(z)
+
+        def last_product(c):
+            lo, hi = Z_CHUNKS[c]
+            z_q = quantize("z%d" % c, z_bf[c][:].rearrange("p n t -> p (n t)"), hi - lo)
+            product(h0_ps[c][:, 0 : hi - lo], (dk_words, dk_scales), 0, z_q)
+            nc.scalar.activation(h_sb[0][:, lo:hi], h0_ps[c][:, 0 : hi - lo], ACT.Copy, scale=0.0625)
+            for t in range(1, PACK):
+                product(h_ps[t - 1][:, lo:hi], (dk_words, dk_scales), t, z_q)
+
+        weigh(0)
+        for c in range(len(Z_CHUNKS)):
+            if c + 1 < len(Z_CHUNKS):
+                weigh(c + 1)
+            last_product(c)
+        for t in range(1, PACK):
+            nc.scalar.activation(h_sb[t][:], h_ps[t - 1][:], ACT.Copy, scale=0.0625)
 
         out_rows = out.rearrange("(p t) n -> t p n", t=PACK)
         for t in range(PACK):

@@ -1,6 +1,7 @@
 from contextlib import ExitStack
 
 import concourse.mybir as mybir
+from concourse.masks import make_identity
 
 F32 = mybir.dt.float32
 BF16 = mybir.dt.bfloat16
@@ -36,6 +37,8 @@ def tile_picked_twqnormbratio_none_p_kernel(tc, x_words, x_scales, w1, w2, gs, d
 
         xs_tab = tile("xs_tab", [P, T], U8)
         nc.gpsimd.memset(xs_tab[:].bitcast(I32), 0)
+        ident = tile("ident", [P, P], F32)
+        make_identity(nc, ident[:])
         warm = tile("warm", [P, 1], F32)
         warm2 = tile("warm2", [P, 1], F32)
         nc.vector.memset(warm[:], 1.0)
@@ -204,18 +207,36 @@ def tile_picked_twqnormbratio_none_p_kernel(tc, x_words, x_scales, w1, w2, gs, d
             nc.scalar.activation(h_sb[t][:], h_ps[t - 1][:], ACT.Copy, scale=0.0625)
 
         out_rows = out.rearrange("(p t) n -> t p n", t=PACK)
+        pa, inv_b, excess = [], [], []
+        turned_tags = ("a0", "b3", "b0", "b1")
+        back_tags = ("b2", "a1", "a2", "a3")
         for t in range(PACK):
             pb = gather("pb%d" % t, h_sb[t], n4_sb, W, F32)
-            pa = gather("pa%d" % t, h_sb[t], n3_sb, W, F32)
+            pa.append(gather("pa%d" % t, h_sb[t], n3_sb, W, F32))
             size = tile("size%d" % t, [P, W], F32)
             nc.scalar.activation(size[:], pb[:], ACT.Abs)
             rt = tile("rt%d" % t, [P, W], F32)
             nc.scalar.activation(rt[:], size[:], ACT.Abs_reciprocal_sqrt, bias=0.5)
-            iv = tile("iv%d" % t, [P, W], F32)
-            nc.scalar.activation(iv[:], rt[:], ACT.Square)
-            rb = tile("rb%d" % t, [P, W], F32)
-            nc.vector.tensor_tensor(rb[:], pa[:], pb[:], ALU.max)
-            res = tile("res%d" % t, [P, S], F32)
-            nc.vector.tensor_copy(res[:].indirect(n4_sb[:]), rb[:])
-            nc.vector.tensor_tensor(res[:].indirect(n3_sb[:]), pa[:], iv[:], ALU.mult)
-            nc.sync.dma_start(out_rows[t], res[:])
+            inv_b.append(tile("inv_b%d" % t, [P, W], F32))
+            nc.scalar.activation(inv_b[t][:], rt[:], ACT.Square)
+            neg_pa = tile("neg_pa%d" % t, [P, W], F32)
+            nc.scalar.activation(neg_pa[:], pa[t][:], ACT.Copy, scale=-1.0)
+            turned = psum.tile([P, W], F32, name="turned%d" % t, tag=turned_tags[t])
+            for u in range(W // P):
+                cols = slice(u * P, (u + 1) * P)
+                nc.tensor.matmul(turned[:, cols], pb[:, cols], ident[:], start=True, stop=False, is_transpose=True)
+                nc.tensor.matmul(turned[:, cols], neg_pa[:, cols], ident[:], start=False, stop=True, is_transpose=True)
+            turned_sb = tile("turned_sb%d" % t, [P, W], F32)
+            nc.scalar.activation(turned_sb[:], turned[:], ACT.Relu)
+            back = psum.tile([P, W], F32, name="back%d" % t, tag=back_tags[t])
+            for u in range(W // P):
+                cols = slice(u * P, (u + 1) * P)
+                nc.tensor.transpose(back[:, cols], turned_sb[:, cols], ident[:])
+            excess.append(tile("excess%d" % t, [P, W], F32))
+            nc.scalar.copy(excess[t][:], back[:])
+        res = [tile("res%d" % t, [P, S], F32) for t in range(PACK)]
+        for t in range(PACK):
+            nc.vector.tensor_tensor(res[t][:].indirect(n3_sb[:]), pa[t][:], inv_b[t][:], ALU.mult)
+        for t in range(PACK):
+            nc.vector.tensor_tensor(res[t][:].indirect(n4_sb[:]), pa[t][:], excess[t][:], ALU.add)
+            nc.sync.dma_start(out_rows[t], res[t][:])

@@ -13,230 +13,249 @@ FP8X4 = mybir.dt.float8_e4m3fn_x4
 ALU = mybir.AluOpType
 ACT = mybir.ActivationFunctionType
 
-P = 128
-PACK = 4
 K, T, S, H, G, W = 512, 1024, 512, 512, 2048, 256
 FLOPS = 3 * 2 * K * H * S
+
+P = 128
+PACK = 4
+TILES = H // P
+QUAD = 32
+GROUP = 16
+LINE = 4
+HALF = S // 2
 Z_CHUNKS = ((0, 256), (256, 384), (384, 512))
 
 
-def tile_picked_twqnormbratio_none_p_kernel(tc, x_words, x_scales, w1, w2, gs, d_words, d_scales, offs, two, n1, n2, k1, n3, n4, out):
+def tile_picked_twqnormbratio_none_p_kernel(
+    tc, x_words, x_scales, w1, w2, gs, d_words, d_scales, offs, two, n1, n2, k1, n3, n4, out
+):
     nc = tc.nc
     with ExitStack() as ctx:
         lists = ctx.enter_context(tc.tile_pool(name="lists", bufs=1))
         sb = ctx.enter_context(tc.tile_pool(name="sb", bufs=1))
         psum = ctx.enter_context(tc.psum_pool(name="psum", bufs=1))
 
-        def tile(name, shape, dtype):
-            return sb.tile(shape, dtype, name=name, align_bytes=64)
+        def tile(name, shape, dtype, tag=None):
+            return sb.tile(shape, dtype, name=name, tag=tag or name, align_bytes=64)
 
         def load_list(name, src):
             dst = lists.tile(list(src.shape), U16, name=name)
             nc.sync.dma_start(dst[:], src)
             return dst
 
-        xs_tab = tile("xs_tab", [P, T], U8)
-        nc.gpsimd.memset(xs_tab[:].bitcast(I32), 0)
-        ident = tile("ident", [P, P], F32)
-        make_identity(nc, ident[:])
-        warm = tile("warm", [P, 1], F32)
-        warm2 = tile("warm2", [P, 1], F32)
-        nc.vector.memset(warm[:], 1.0)
-        nc.scalar.activation(warm2[:], warm[:], ACT.Abs_reciprocal_sqrt)
-        ds_tab = tile("ds_tab", [P, G], U8)
-        nc.vector.memset(ds_tab[:].bitcast(I32), 0)
-
         def load_half(name, w, u):
             raw = tile("%s_raw%d" % (name, u), [P, PACK, H // 2], F32)
-            nc.sync.dma_start(raw[:], w.rearrange("(p j) c -> p j c", j=PACK)[:, :, u * 256 : (u + 1) * 256])
+            nc.sync.dma_start(raw[:], w.rearrange("(p j) c -> p j c", j=PACK)[:, :, u * (H // 2) : (u + 1) * (H // 2)])
             return raw
 
-        two_sb = load_list("two_sb", two)
-        offs_sb = load_list("offs_sb", offs)
-        for q in range(4):
-            nc.sync.dma_start(xs_tab[32 * q : 32 * q + 4, :].bitcast(I32), x_scales[0, 4 * q : 4 * q + 4, :].bitcast(I32))
-        w2_raw = [load_half("w2", w2, 0)]
-        xw_tab = tile("xw_tab", [P, T], U32)
-        nc.sync.dma_start(xw_tab[:].bitcast(I32), x_words[0].rearrange("p n r -> p (n r)").bitcast(I32))
-        w2_raw.append(load_half("w2", w2, 1))
-        w1_raw = [load_half("w1", w1, 0)]
-        k1_sb = load_list("k1_sb", k1)
-        for s in range(2):
-            nc.sync.dma_start(ds_tab[s:P:16, :].bitcast(I32), d_scales[0, s:16:2, :].bitcast(I32))
-        w1_raw.append(load_half("w1", w1, 1))
-        n2_sb = load_list("n2_sb", n2)
-        gs_sb = tile("gs_sb", [P, PACK], F32)
-        nc.sync.dma_start(gs_sb[:], gs.rearrange("(p t) o -> p (t o)", t=PACK))
-        dw_tab = tile("dw_tab", [P, G], U32)
-        nc.sync.dma_start(dw_tab[:].bitcast(I32), d_words[0].rearrange("p n r -> p (n r)").bitcast(I32))
-        n1_sb = load_list("n1_sb", n1)
-        n3_sb = load_list("n3_sb", n3)
-        n4_sb = load_list("n4_sb", n4)
-        neg_gs = tile("neg_gs", [P, PACK], F32)
-        nc.gpsimd.tensor_scalar(neg_gs[:], gs_sb[:], -1.0, 0.0, ALU.mult, ALU.add)
-
-        def gather(name, table, offsets, n, dtype):
+        def gather(name, window, offsets, n, dtype):
             dst = tile(name, [P, n], dtype)
-            nc.vector.tensor_copy(dst[:], table[:].indirect(offsets[:]))
+            nc.vector.tensor_copy(dst[:], window[:].indirect(offsets[:]))
             return dst
 
-        x2_scales = gather("x2_scales", xs_tab, two_sb, S, U8)
-        x1_scales = gather("x1_scales", xs_tab, offs_sb, S, U8)
-        x2_words = gather("x2_words", xw_tab, two_sb, S, U32)
-        x1_words = gather("x1_words", xw_tab, offs_sb, S, U32)
-
         def round_weight(name, halves):
-            wb = tile(name + "_bf", [P, PACK, P, PACK], BF16)
+            rounded = tile(name + "_bf", [P, TILES, P, PACK], BF16)
             for u in range(2):
                 nc.scalar.copy(
-                    wb[:, :, u * 64 : (u + 1) * 64, :].rearrange("p t m j -> p m j t"),
-                    halves[u][:].rearrange("p j (m t) -> p m j t", t=PACK),
+                    rounded[:, :, u * (P // 2) : (u + 1) * (P // 2), :].rearrange("p t m j -> p m j t"),
+                    halves[u][:].rearrange("p j (m t) -> p m j t", t=TILES),
                 )
-            return wb[:].rearrange("p t m j -> p (t m j)")
-
-        w2_bf = round_weight("w2", w2_raw)
-        w1_bf = round_weight("w1", w1_raw)
+            return rounded[:].rearrange("p t m j -> p (t m j)")
 
         def quantize(name, src, n):
-            codes = tile(name + "_codes", [P, n], U32)
+            words = tile(name + "_words", [P, n], U32)
             scales = tile(name + "_scales", [P, n], U8)
-            nc.vector.quantize_mx(out=codes[:].bitcast(FP8X4), scales=scales[:], in_=src)
-            return codes, scales
+            nc.vector.quantize_mx(out=words[:].bitcast(FP8X4), scales=scales[:], in_=src)
+            return words, scales
 
-        def product(dst, lhs, t, rhs):
-            cols = slice(t * P, (t + 1) * P)
+        def block(src, b):
+            return src[:, b * P : (b + 1) * P]
+
+        def product(dst, lhs_words, lhs_scales, rhs):
             nc.tensor.matmul_mx(
                 out=dst,
-                lhsT=lhs[0][:, cols].bitcast(FP8X4),
-                lhsT_scale=lhs[1][:, cols],
+                lhsT=lhs_words.bitcast(FP8X4),
+                lhsT_scale=lhs_scales,
                 rhs=rhs[0][:].bitcast(FP8X4),
                 rhs_scale=rhs[1][:],
                 start=True,
                 stop=True,
             )
 
+        xs_table = tile("xs_table", [P, T], U8)
+        nc.gpsimd.memset(xs_table[:].bitcast(I32), 0)
+        ident = tile("ident", [P, P], F32)
+        make_identity(nc, ident[:])
+        warm_in = tile("warm_in", [P, 1], F32)
+        warm_out = tile("warm_out", [P, 1], F32)
+        nc.vector.memset(warm_in[:], 1.0)
+        nc.scalar.activation(warm_out[:], warm_in[:], ACT.Abs_reciprocal_sqrt)
+        ds_table = tile("ds_table", [P, G], U8)
+        nc.vector.memset(ds_table[:].bitcast(I32), 0)
+
+        two_sb = load_list("two_sb", two)
+        offs_sb = load_list("offs_sb", offs)
+        for q in range(P // QUAD):
+            nc.sync.dma_start(
+                xs_table[QUAD * q : QUAD * q + 4, :].bitcast(I32), x_scales[0, 4 * q : 4 * q + 4, :].bitcast(I32)
+            )
+        w2_raw = [load_half("w2", w2, 0)]
+        xw_table = tile("xw_table", [P, T], U32)
+        nc.sync.dma_start(xw_table[:].bitcast(I32), x_words[0].rearrange("p n j -> p (n j)").bitcast(I32))
+        w2_raw.append(load_half("w2", w2, 1))
+        w1_raw = [load_half("w1", w1, 0)]
+        k1_sb = load_list("k1_sb", k1)
+        for s in range(2):
+            nc.sync.dma_start(ds_table[s:P:GROUP, :].bitcast(I32), d_scales[0, s:16:2, :].bitcast(I32))
+        w1_raw.append(load_half("w1", w1, 1))
+        n2_sb = load_list("n2_sb", n2)
+        gs_sb = tile("gs_sb", [P, TILES], F32)
+        nc.sync.dma_start(gs_sb[:], gs.rearrange("(p t) o -> p (t o)", t=TILES))
+        dw_table = tile("dw_table", [P, G], U32)
+        nc.sync.dma_start(dw_table[:].bitcast(I32), d_words[0].rearrange("p n j -> p (n j)").bitcast(I32))
+        n1_sb = load_list("n1_sb", n1)
+        n3_sb = load_list("n3_sb", n3)
+        n4_sb = load_list("n4_sb", n4)
+        neg_gs = tile("neg_gs", [P, TILES], F32)
+        nc.gpsimd.tensor_scalar(neg_gs[:], gs_sb[:], -1.0, 0.0, ALU.mult, ALU.add)
+
+        x2_scales = gather("x2_scales", xs_table, two_sb, S, U8)
+        x1_scales = gather("x1_scales", xs_table, offs_sb, S, U8)
+        x2_words = gather("x2_words", xw_table, two_sb, S, U32)
+        x1_words = gather("x1_words", xw_table, offs_sb, S, U32)
+        w2_bf = round_weight("w2", w2_raw)
+        w1_bf = round_weight("w1", w1_raw)
+
+        lookups = 2 * TILES
+        windows = [tile("window%d" % g, [P, S if g in (0, lookups) else 2 * S], F32) for g in range(lookups + 1)]
+
         def own(g):
             return windows[g][:, 0:S]
 
-        def spare(g):
-            return windows[g + 1][:, (0 if g == 7 else S) :]
+        def twin(g):
+            return windows[g + 1][:, (0 if g + 1 == lookups else S) :]
 
-        windows = [tile("win%d" % g, [P, S if g in (0, 8) else 2 * S], F32) for g in range(9)]
+        halves = (slice(0, HALF), slice(HALF, S))
+
         w2_q = quantize("w2", w2_bf, H)
-        d_ps = [psum.tile([P, S], F32, name="d_ps%d" % t, tag="a%d" % t) for t in range(PACK)]
-        for t in range(PACK):
-            product(d_ps[t][:], w2_q, t, (x2_words, x2_scales))
-        for t in range(PACK):
+        d_ps = [psum.tile([P, S], F32, name="d_ps%d" % t, tag="a%d" % t) for t in range(TILES)]
+        for t in range(TILES):
+            product(d_ps[t][:], block(w2_q[0], t), block(w2_q[1], t), (x2_words, x2_scales))
+        for t in range(TILES):
             nc.scalar.activation(own(t), d_ps[t][:], ACT.Abs)
-            nc.scalar.activation(spare(t), d_ps[t][:], ACT.Abs)
+            for cols in halves if t == 0 else (slice(0, S),):
+                nc.scalar.activation(twin(t)[:, cols], d_ps[t][:, cols], ACT.Abs)
 
-        dk_raw_scales = gather("dk_raw_scales", ds_tab, k1_sb, H, U8)
+        dk_picked_scales = gather("dk_picked_scales", ds_table, k1_sb, H, U8)
         dk_scales = tile("dk_scales", [P, H], U8)
         nc.vector.tensor_copy(
-            dk_scales[:].rearrange("p (t m) -> p m t", t=PACK), dk_raw_scales[:].rearrange("p (m t) -> p m t", t=PACK)
+            dk_scales[:].rearrange("p (t m) -> p m t", t=TILES),
+            dk_picked_scales[:].rearrange("p (m t) -> p m t", t=TILES),
         )
         for s in range(2):
-            nc.sync.dma_start(dk_scales[2 + s : P : 32, :].bitcast(I32), dk_scales[16 + s : P : 32, :].bitcast(I32))
+            nc.sync.dma_start(
+                dk_scales[2 + s : P : QUAD, :].bitcast(I32), dk_scales[GROUP + s : P : QUAD, :].bitcast(I32)
+            )
 
         w1_q = quantize("w1", w1_bf, H)
-        y_ps = [psum.tile([P, S], F32, name="y_ps%d" % t, tag="b%d" % t) for t in range(PACK)]
-        for t in range(PACK):
-            product(y_ps[t][:], w1_q, t, (x1_words, x1_scales))
+        y_ps = [psum.tile([P, S], F32, name="y_ps%d" % t, tag="b%d" % t) for t in range(TILES)]
+        for t in range(TILES):
+            product(y_ps[t][:], block(w1_q[0], t), block(w1_q[1], t), (x1_words, x1_scales))
 
-        dk_raw_words = gather("dk_raw_words", dw_tab, k1_sb, H, U32)
-        dk_words = tile("dk_words", [P, H], U32)
-        nc.vector.tensor_copy(
-            dk_words[:].rearrange("p (t m) -> p m t", t=PACK), dk_raw_words[:].rearrange("p (m t) -> p m t", t=PACK)
-        )
+        dk_picked_words = gather("dk_picked_words", dw_table, k1_sb, H, U32)
+        dk_by_tile = dk_picked_words[:].rearrange("p (m t) -> p m t", t=TILES)
+        dk_words_first = tile("dk_words_first", [P, P], U32)
+        nc.vector.tensor_copy(dk_words_first[:], dk_by_tile[:, :, 0])
 
-        den = tile("den", [P, PACK, S], F32)
-        root = tile("root", [P, PACK, S], F32)
-        inv = tile("inv", [P, PACK, S], F32)
-        num = tile("num", [P, PACK, S], F32)
-        for t in range(PACK):
+        den = tile("den", [P, TILES, S], F32)
+        root = tile("root", [P, TILES, S], F32)
+        inv = tile("inv", [P, TILES, S], F32)
+        num = tile("num", [P, TILES, S], F32)
+        for u, cols in enumerate(halves):
+            half_list = n2_sb[:, u * (HALF // GROUP) : (u + 1) * (HALF // GROUP)]
+            nc.vector.tensor_tensor(den[:, 0, cols], windows[0][:].indirect(half_list), twin(0)[:, cols], ALU.add)
+        for t in range(1, TILES):
+            nc.vector.tensor_tensor(den[:, t, :], windows[t][:].indirect(n2_sb[:]), twin(t), ALU.add)
+        for t in range(TILES):
+            nc.scalar.activation(own(TILES + t), y_ps[t][:], ACT.Copy, scale=neg_gs[:, t : t + 1])
             if t == 0:
-                for u in range(2):
-                    cols = slice(u * 256, (u + 1) * 256)
-                    nc.vector.tensor_tensor(
-                        den[:, t, cols], windows[t][:].indirect(n2_sb[:, u * 16 : (u + 1) * 16]), spare(t)[:, cols], ALU.add
-                    )
+                nc.scalar.activation(twin(TILES + t), y_ps[t][:], ACT.Copy, scale=neg_gs[:, t : t + 1])
             else:
-                nc.vector.tensor_tensor(den[:, t, :], windows[t][:].indirect(n2_sb[:]), spare(t), ALU.add)
-        for t in range(PACK):
-            nc.scalar.activation(own(PACK + t), y_ps[t][:], ACT.Copy, scale=neg_gs[:, t : t + 1])
-            if t == 0:
-                nc.scalar.activation(spare(PACK + t), y_ps[t][:], ACT.Copy, scale=neg_gs[:, t : t + 1])
-            else:
-                nc.sync.dma_start(spare(PACK + t), own(PACK + t))
-        for t in range(PACK):
+                nc.sync.dma_start(twin(TILES + t), own(TILES + t))
+        for t in range(TILES):
             nc.scalar.activation(root[:, t, :], den[:, t, :], ACT.Abs_reciprocal_sqrt, bias=0.5)
             nc.scalar.activation(inv[:, t, :], root[:, t, :], ACT.Square)
-        for t in range(PACK):
-            nc.vector.tensor_tensor(num[:, t, :], windows[PACK + t][:].indirect(n1_sb[:]), spare(PACK + t), ALU.subtract)
-
-        h_ps = [psum.tile([P, S], F32, name="h_ps%d" % t, tag="a%d" % t) for t in range(1, PACK)]
-        h0_ps = [psum.tile([P, S], F32, name="h0_ps%d" % c, tag="b%d" % c) for c in range(len(Z_CHUNKS))]
-        h_sb = [tile("h_sb%d" % t, [P, S], F32) for t in range(PACK)]
-        z_bf = []
-
-        def weigh(c):
-            lo, hi = Z_CHUNKS[c]
-            z = tile("z_bf%d" % c, [P, hi - lo, PACK], BF16)
+        for t in range(TILES):
             nc.vector.tensor_tensor(
-                z[:].rearrange("p (c i) t -> p c t i", i=4),
-                num[:, :, lo:hi].rearrange("p t (c i) -> p c t i", i=4),
-                inv[:, :, lo:hi].rearrange("p t (c i) -> p c t i", i=4),
+                num[:, t, :], windows[TILES + t][:].indirect(n1_sb[:]), twin(TILES + t), ALU.subtract
+            )
+
+        h_rest_ps = [psum.tile([P, S], F32, name="h_ps%d" % t, tag="a%d" % t) for t in range(1, TILES)]
+        h_first_ps = [psum.tile([P, S], F32, name="h0_ps%d" % c, tag="b%d" % c) for c in range(len(Z_CHUNKS))]
+        h_sb = [tile("h_sb%d" % t, [P, S], F32) for t in range(TILES)]
+        z_bf, z_q = [], []
+
+        def make_z(c):
+            lo, hi = Z_CHUNKS[c]
+            z = tile("z_bf%d" % c, [P, hi - lo, TILES], BF16)
+            nc.vector.tensor_tensor(
+                z[:].rearrange("p (c i) t -> p c t i", i=LINE),
+                num[:, :, lo:hi].rearrange("p t (c i) -> p c t i", i=LINE),
+                inv[:, :, lo:hi].rearrange("p t (c i) -> p c t i", i=LINE),
                 ALU.mult,
             )
             z_bf.append(z)
 
-        def last_product(c):
+        def first_tile_of_h(c):
             lo, hi = Z_CHUNKS[c]
-            z_q = quantize("z%d" % c, z_bf[c][:].rearrange("p n t -> p (n t)"), hi - lo)
-            product(h0_ps[c][:, 0 : hi - lo], (dk_words, dk_scales), 0, z_q)
-            nc.scalar.activation(h_sb[0][:, lo:hi], h0_ps[c][:, 0 : hi - lo], ACT.Copy, scale=0.0625)
-            for t in range(1, PACK):
-                product(h_ps[t - 1][:, lo:hi], (dk_words, dk_scales), t, z_q)
+            z_q.append(quantize("z%d" % c, z_bf[c][:].rearrange("p n t -> p (n t)"), hi - lo))
+            product(h_first_ps[c][:, 0 : hi - lo], dk_words_first[:], block(dk_scales, 0), z_q[c])
+            nc.scalar.activation(h_sb[0][:, lo:hi], h_first_ps[c][:, 0 : hi - lo], ACT.Copy, scale=0.0625)
 
-        weigh(0)
+        make_z(0)
         for c in range(len(Z_CHUNKS)):
             if c + 1 < len(Z_CHUNKS):
-                weigh(c + 1)
-            last_product(c)
-        for t in range(1, PACK):
-            nc.scalar.activation(h_sb[t][:], h_ps[t - 1][:], ACT.Copy, scale=0.0625)
+                make_z(c + 1)
+            first_tile_of_h(c)
+        dk_words_rest = tile("dk_words_rest", [P, H - P], U32, tag="z_bf%d" % (len(Z_CHUNKS) - 1))
+        nc.vector.tensor_copy(dk_words_rest[:].rearrange("p (t m) -> p m t", t=TILES - 1), dk_by_tile[:, :, 1:TILES])
+        for t in range(1, TILES):
+            for c, (lo, hi) in enumerate(Z_CHUNKS):
+                product(h_rest_ps[t - 1][:, lo:hi], block(dk_words_rest, t - 1), block(dk_scales, t), z_q[c])
+            nc.scalar.activation(h_sb[t][:], h_rest_ps[t - 1][:], ACT.Copy, scale=0.0625)
 
-        out_rows = out.rearrange("(p t) n -> t p n", t=PACK)
+        out_rows = out.rearrange("(p t) n -> t p n", t=TILES)
         pa, inv_b, excess = [], [], []
-        turned_tags = ("a0", "b3", "b0", "b1")
-        back_tags = ("b2", "a1", "a2", "a3")
-        for t in range(PACK):
+        turned_banks = ("a0", "b3", "b0", "b1")
+        back_banks = ("b2", "a1", "a2", "a3")
+        for t in range(TILES):
             pb = gather("pb%d" % t, h_sb[t], n4_sb, W, F32)
             pa.append(gather("pa%d" % t, h_sb[t], n3_sb, W, F32))
-            size = tile("size%d" % t, [P, W], F32)
-            nc.scalar.activation(size[:], pb[:], ACT.Abs)
-            rt = tile("rt%d" % t, [P, W], F32)
-            nc.scalar.activation(rt[:], size[:], ACT.Abs_reciprocal_sqrt, bias=0.5)
+            size_b = tile("size_b%d" % t, [P, W], F32)
+            nc.scalar.activation(size_b[:], pb[:], ACT.Abs)
+            root_b = tile("root_b%d" % t, [P, W], F32)
+            nc.scalar.activation(root_b[:], size_b[:], ACT.Abs_reciprocal_sqrt, bias=0.5)
             inv_b.append(tile("inv_b%d" % t, [P, W], F32))
-            nc.scalar.activation(inv_b[t][:], rt[:], ACT.Square)
+            nc.scalar.activation(inv_b[t][:], root_b[:], ACT.Square)
             neg_pa = tile("neg_pa%d" % t, [P, W], F32)
             nc.scalar.activation(neg_pa[:], pa[t][:], ACT.Copy, scale=-1.0)
-            turned = psum.tile([P, W], F32, name="turned%d" % t, tag=turned_tags[t])
-            for u in range(W // P):
-                cols = slice(u * P, (u + 1) * P)
-                nc.tensor.matmul(turned[:, cols], pb[:, cols], ident[:], start=True, stop=False, is_transpose=True)
-                nc.tensor.matmul(turned[:, cols], neg_pa[:, cols], ident[:], start=False, stop=True, is_transpose=True)
+            turned_ps = psum.tile([P, W], F32, name="turned_ps%d" % t, tag=turned_banks[t])
+            for b in range(W // P):
+                nc.tensor.matmul(block(turned_ps, b), block(pb, b), ident[:], start=True, stop=False, is_transpose=True)
+                nc.tensor.matmul(
+                    block(turned_ps, b), block(neg_pa, b), ident[:], start=False, stop=True, is_transpose=True
+                )
             turned_sb = tile("turned_sb%d" % t, [P, W], F32)
-            nc.scalar.activation(turned_sb[:], turned[:], ACT.Relu)
-            back = psum.tile([P, W], F32, name="back%d" % t, tag=back_tags[t])
-            for u in range(W // P):
-                cols = slice(u * P, (u + 1) * P)
-                nc.tensor.transpose(back[:, cols], turned_sb[:, cols], ident[:])
+            nc.scalar.activation(turned_sb[:], turned_ps[:], ACT.Relu)
+            back_ps = psum.tile([P, W], F32, name="back_ps%d" % t, tag=back_banks[t])
+            for b in range(W // P):
+                nc.tensor.transpose(block(back_ps, b), block(turned_sb, b), ident[:])
             excess.append(tile("excess%d" % t, [P, W], F32))
-            nc.scalar.copy(excess[t][:], back[:])
-        res = [tile("res%d" % t, [P, S], F32) for t in range(PACK)]
-        for t in range(PACK):
+            nc.scalar.copy(excess[t][:], back_ps[:])
+
+        res = [tile("res%d" % t, [P, S], F32) for t in range(TILES)]
+        for t in range(TILES):
             nc.vector.tensor_tensor(res[t][:].indirect(n3_sb[:]), pa[t][:], inv_b[t][:], ALU.mult)
-        for t in range(PACK):
+        for t in range(TILES):
             nc.vector.tensor_tensor(res[t][:].indirect(n4_sb[:]), pa[t][:], excess[t][:], ALU.add)
             nc.sync.dma_start(out_rows[t], res[t][:])

from contextlib import ExitStack

import concourse.mybir as mybir
from concourse.masks import make_identity

F32 = mybir.dt.float32
BF16 = mybir.dt.bfloat16
I32 = mybir.dt.int32
U32 = mybir.dt.uint32
U16 = mybir.dt.uint16
U8 = mybir.dt.uint8
FP8X4 = mybir.dt.float8_e4m3fn_x4
ALU = mybir.AluOpType
ACT = mybir.ActivationFunctionType

K, T, S, H, G, W = 512, 1024, 512, 512, 2048, 256
FLOPS = 3 * 2 * K * H * S

P = 128
PACK = 4
TILES = H // P
QUAD = 32
GROUP = 16
LINE = 4
HALF = S // 2
Z_CHUNKS = ((0, 256), (256, 384), (384, 512))


def tile_picked_twqnormbratio_none_p_kernel(
    tc, x_words, x_scales, w1, w2, gs, d_words, d_scales, offs, two, n1, n2, k1, n3, n4, out
):
    nc = tc.nc
    with ExitStack() as ctx:
        lists = ctx.enter_context(tc.tile_pool(name="lists", bufs=1))
        sb = ctx.enter_context(tc.tile_pool(name="sb", bufs=1))
        psum = ctx.enter_context(tc.psum_pool(name="psum", bufs=1))

        def tile(name, shape, dtype, tag=None):
            return sb.tile(shape, dtype, name=name, tag=tag or name, align_bytes=64)

        def load_list(name, src):
            dst = lists.tile(list(src.shape), U16, name=name)
            nc.sync.dma_start(dst[:], src)
            return dst

        def load_half(name, w, u):
            raw = tile("%s_raw%d" % (name, u), [P, PACK, H // 2], F32)
            nc.sync.dma_start(raw[:], w.rearrange("(p j) c -> p j c", j=PACK)[:, :, u * (H // 2) : (u + 1) * (H // 2)])
            return raw

        def gather(name, window, offsets, n, dtype):
            dst = tile(name, [P, n], dtype)
            nc.vector.tensor_copy(dst[:], window[:].indirect(offsets[:]))
            return dst

        def round_weight(name, halves):
            rounded = tile(name + "_bf", [P, TILES, P, PACK], BF16)
            for u in range(2):
                nc.scalar.copy(
                    rounded[:, :, u * (P // 2) : (u + 1) * (P // 2), :].rearrange("p t m j -> p m j t"),
                    halves[u][:].rearrange("p j (m t) -> p m j t", t=TILES),
                )
            return rounded[:].rearrange("p t m j -> p (t m j)")

        def quantize(name, src, n):
            words = tile(name + "_words", [P, n], U32)
            scales = tile(name + "_scales", [P, n], U8)
            nc.vector.quantize_mx(out=words[:].bitcast(FP8X4), scales=scales[:], in_=src)
            return words, scales

        def block(src, b):
            return src[:, b * P : (b + 1) * P]

        def product(dst, lhs_words, lhs_scales, rhs):
            nc.tensor.matmul_mx(
                out=dst,
                lhsT=lhs_words.bitcast(FP8X4),
                lhsT_scale=lhs_scales,
                rhs=rhs[0][:].bitcast(FP8X4),
                rhs_scale=rhs[1][:],
                start=True,
                stop=True,
            )

        xs_table = tile("xs_table", [P, T], U8)
        nc.gpsimd.memset(xs_table[:].bitcast(I32), 0)
        ident = tile("ident", [P, P], F32)
        make_identity(nc, ident[:])
        warm_in = tile("warm_in", [P, 1], F32)
        warm_out = tile("warm_out", [P, 1], F32)
        nc.vector.memset(warm_in[:], 1.0)
        nc.scalar.activation(warm_out[:], warm_in[:], ACT.Abs_reciprocal_sqrt)
        ds_table = tile("ds_table", [P, G], U8)
        nc.vector.memset(ds_table[:].bitcast(I32), 0)

        two_sb = load_list("two_sb", two)
        offs_sb = load_list("offs_sb", offs)
        for q in range(P // QUAD):
            nc.sync.dma_start(
                xs_table[QUAD * q : QUAD * q + 4, :].bitcast(I32), x_scales[0, 4 * q : 4 * q + 4, :].bitcast(I32)
            )
        w2_raw = [load_half("w2", w2, 0)]
        xw_table = tile("xw_table", [P, T], U32)
        nc.sync.dma_start(xw_table[:].bitcast(I32), x_words[0].rearrange("p n j -> p (n j)").bitcast(I32))
        w2_raw.append(load_half("w2", w2, 1))
        w1_raw = [load_half("w1", w1, 0)]
        k1_sb = load_list("k1_sb", k1)
        for s in range(2):
            nc.sync.dma_start(ds_table[s:P:GROUP, :].bitcast(I32), d_scales[0, s:16:2, :].bitcast(I32))
        w1_raw.append(load_half("w1", w1, 1))
        n2_sb = load_list("n2_sb", n2)
        gs_sb = tile("gs_sb", [P, TILES], F32)
        nc.sync.dma_start(gs_sb[:], gs.rearrange("(p t) o -> p (t o)", t=TILES))
        dw_table = tile("dw_table", [P, G], U32)
        nc.sync.dma_start(dw_table[:].bitcast(I32), d_words[0].rearrange("p n j -> p (n j)").bitcast(I32))
        n1_sb = load_list("n1_sb", n1)
        n3_sb = load_list("n3_sb", n3)
        n4_sb = load_list("n4_sb", n4)
        neg_gs = tile("neg_gs", [P, TILES], F32)
        nc.gpsimd.tensor_scalar(neg_gs[:], gs_sb[:], -1.0, 0.0, ALU.mult, ALU.add)

        x2_scales = gather("x2_scales", xs_table, two_sb, S, U8)
        x1_scales = gather("x1_scales", xs_table, offs_sb, S, U8)
        x2_words = gather("x2_words", xw_table, two_sb, S, U32)
        x1_words = gather("x1_words", xw_table, offs_sb, S, U32)
        w2_bf = round_weight("w2", w2_raw)
        w1_bf = round_weight("w1", w1_raw)

        lookups = 2 * TILES
        windows = [tile("window%d" % g, [P, S if g in (0, lookups) else 2 * S], F32) for g in range(lookups + 1)]

        def own(g):
            return windows[g][:, 0:S]

        def twin(g):
            return windows[g + 1][:, (0 if g + 1 == lookups else S) :]

        halves = (slice(0, HALF), slice(HALF, S))

        w2_q = quantize("w2", w2_bf, H)
        d_ps = [psum.tile([P, S], F32, name="d_ps%d" % t, tag="a%d" % t) for t in range(TILES)]
        for t in range(TILES):
            product(d_ps[t][:], block(w2_q[0], t), block(w2_q[1], t), (x2_words, x2_scales))
        for t in range(TILES):
            nc.scalar.activation(own(t), d_ps[t][:], ACT.Abs)
            for cols in halves if t == 0 else (slice(0, S),):
                nc.scalar.activation(twin(t)[:, cols], d_ps[t][:, cols], ACT.Abs)

        dk_picked_scales = gather("dk_picked_scales", ds_table, k1_sb, H, U8)
        dk_scales = tile("dk_scales", [P, H], U8)
        nc.vector.tensor_copy(
            dk_scales[:].rearrange("p (t m) -> p m t", t=TILES),
            dk_picked_scales[:].rearrange("p (m t) -> p m t", t=TILES),
        )
        for s in range(2):
            nc.sync.dma_start(
                dk_scales[2 + s : P : QUAD, :].bitcast(I32), dk_scales[GROUP + s : P : QUAD, :].bitcast(I32)
            )

        w1_q = quantize("w1", w1_bf, H)
        y_ps = [psum.tile([P, S], F32, name="y_ps%d" % t, tag="b%d" % t) for t in range(TILES)]
        for t in range(TILES):
            product(y_ps[t][:], block(w1_q[0], t), block(w1_q[1], t), (x1_words, x1_scales))

        dk_picked_words = gather("dk_picked_words", dw_table, k1_sb, H, U32)
        dk_by_tile = dk_picked_words[:].rearrange("p (m t) -> p m t", t=TILES)
        dk_words_first = tile("dk_words_first", [P, P], U32)
        nc.vector.tensor_copy(dk_words_first[:], dk_by_tile[:, :, 0])

        den = tile("den", [P, TILES, S], F32)
        root = tile("root", [P, TILES, S], F32)
        inv = tile("inv", [P, TILES, S], F32)
        num = tile("num", [P, TILES, S], F32)
        for u, cols in enumerate(halves):
            half_list = n2_sb[:, u * (HALF // GROUP) : (u + 1) * (HALF // GROUP)]
            nc.vector.tensor_tensor(den[:, 0, cols], windows[0][:].indirect(half_list), twin(0)[:, cols], ALU.add)
        for t in range(1, TILES):
            nc.vector.tensor_tensor(den[:, t, :], windows[t][:].indirect(n2_sb[:]), twin(t), ALU.add)
        for t in range(TILES):
            nc.scalar.activation(own(TILES + t), y_ps[t][:], ACT.Copy, scale=neg_gs[:, t : t + 1])
            if t == 0:
                nc.scalar.activation(twin(TILES + t), y_ps[t][:], ACT.Copy, scale=neg_gs[:, t : t + 1])
            else:
                nc.sync.dma_start(twin(TILES + t), own(TILES + t))
        for t in range(TILES):
            nc.scalar.activation(root[:, t, :], den[:, t, :], ACT.Abs_reciprocal_sqrt, bias=0.5)
            nc.scalar.activation(inv[:, t, :], root[:, t, :], ACT.Square)
        for t in range(TILES):
            nc.vector.tensor_tensor(
                num[:, t, :], windows[TILES + t][:].indirect(n1_sb[:]), twin(TILES + t), ALU.subtract
            )

        h_rest_ps = [psum.tile([P, S], F32, name="h_ps%d" % t, tag="a%d" % t) for t in range(1, TILES)]
        h_first_ps = [psum.tile([P, S], F32, name="h0_ps%d" % c, tag="b%d" % c) for c in range(len(Z_CHUNKS))]
        h_sb = [tile("h_sb%d" % t, [P, S], F32) for t in range(TILES)]
        z_bf, z_q = [], []

        def make_z(c):
            lo, hi = Z_CHUNKS[c]
            z = tile("z_bf%d" % c, [P, hi - lo, TILES], BF16)
            nc.vector.tensor_tensor(
                z[:].rearrange("p (c i) t -> p c t i", i=LINE),
                num[:, :, lo:hi].rearrange("p t (c i) -> p c t i", i=LINE),
                inv[:, :, lo:hi].rearrange("p t (c i) -> p c t i", i=LINE),
                ALU.mult,
            )
            z_bf.append(z)

        def first_tile_of_h(c):
            lo, hi = Z_CHUNKS[c]
            z_q.append(quantize("z%d" % c, z_bf[c][:].rearrange("p n t -> p (n t)"), hi - lo))
            product(h_first_ps[c][:, 0 : hi - lo], dk_words_first[:], block(dk_scales, 0), z_q[c])
            nc.scalar.activation(h_sb[0][:, lo:hi], h_first_ps[c][:, 0 : hi - lo], ACT.Copy, scale=0.0625)

        make_z(0)
        for c in range(len(Z_CHUNKS)):
            if c + 1 < len(Z_CHUNKS):
                make_z(c + 1)
            first_tile_of_h(c)
        dk_words_rest = tile("dk_words_rest", [P, H - P], U32, tag="z_bf%d" % (len(Z_CHUNKS) - 1))
        nc.vector.tensor_copy(dk_words_rest[:].rearrange("p (t m) -> p m t", t=TILES - 1), dk_by_tile[:, :, 1:TILES])
        for t in range(1, TILES):
            for c, (lo, hi) in enumerate(Z_CHUNKS):
                product(h_rest_ps[t - 1][:, lo:hi], block(dk_words_rest, t - 1), block(dk_scales, t), z_q[c])
            nc.scalar.activation(h_sb[t][:], h_rest_ps[t - 1][:], ACT.Copy, scale=0.0625)

        out_rows = out.rearrange("(p t) n -> t p n", t=TILES)
        pa, inv_b, excess = [], [], []
        turned_banks = ("a0", "b3", "b0", "b1")
        back_banks = ("b2", "a1", "a2", "a3")
        for t in range(TILES):
            pb = gather("pb%d" % t, h_sb[t], n4_sb, W, F32)
            pa.append(gather("pa%d" % t, h_sb[t], n3_sb, W, F32))
            size_b = tile("size_b%d" % t, [P, W], F32)
            nc.scalar.activation(size_b[:], pb[:], ACT.Abs)
            root_b = tile("root_b%d" % t, [P, W], F32)
            nc.scalar.activation(root_b[:], size_b[:], ACT.Abs_reciprocal_sqrt, bias=0.5)
            inv_b.append(tile("inv_b%d" % t, [P, W], F32))
            nc.scalar.activation(inv_b[t][:], root_b[:], ACT.Square)
            neg_pa = tile("neg_pa%d" % t, [P, W], F32)
            nc.scalar.activation(neg_pa[:], pa[t][:], ACT.Copy, scale=-1.0)
            turned_ps = psum.tile([P, W], F32, name="turned_ps%d" % t, tag=turned_banks[t])
            for b in range(W // P):
                nc.tensor.matmul(block(turned_ps, b), block(pb, b), ident[:], start=True, stop=False, is_transpose=True)
                nc.tensor.matmul(
                    block(turned_ps, b), block(neg_pa, b), ident[:], start=False, stop=True, is_transpose=True
                )
            turned_sb = tile("turned_sb%d" % t, [P, W], F32)
            nc.scalar.activation(turned_sb[:], turned_ps[:], ACT.Relu)
            back_ps = psum.tile([P, W], F32, name="back_ps%d" % t, tag=back_banks[t])
            for b in range(W // P):
                nc.tensor.transpose(block(back_ps, b), block(turned_sb, b), ident[:])
            excess.append(tile("excess%d" % t, [P, W], F32))
            nc.scalar.copy(excess[t][:], back_ps[:])

        res = [tile("res%d" % t, [P, S], F32) for t in range(TILES)]
        for t in range(TILES):
            nc.vector.tensor_tensor(res[t][:].indirect(n3_sb[:]), pa[t][:], inv_b[t][:], ALU.mult)
        for t in range(TILES):
            nc.vector.tensor_tensor(res[t][:].indirect(n4_sb[:]), pa[t][:], excess[t][:], ALU.add)
            nc.sync.dma_start(out_rows[t], res[t][:])
